import numpy as np
import ml_dtypes


def mxq(x, axis, fmt="e4m3"):
    dtype, down = {"e4m3": (ml_dtypes.float8_e4m3fn, 7), "e5m2": (ml_dtypes.float8_e5m2, 14)}[fmt]
    v = np.moveaxis(np.asarray(x, np.float32).astype(ml_dtypes.bfloat16).astype(np.float64), axis, -1)
    blocks = v.reshape(v.shape[:-1] + (-1, 32))
    amax = np.abs(blocks).max(-1, keepdims=True)
    byte = np.maximum(np.where(amax > 0, np.frexp(amax)[1] - 1 + 127, 0) - down, 1)
    scale = np.exp2(byte - 127.0)
    codes = (blocks / scale).astype(np.float32).astype(dtype).astype(np.float64)
    return np.moveaxis((codes * scale).reshape(v.shape), -1, axis)


WIDE = False


def mx_kscale(k):
    if not WIDE:
        return np.ones(k)
    levels = np.array([10, -10, 5, -5, 0])
    if k % 512:
        return np.exp2(np.random.permutation(np.resize(levels, k // 32))).repeat(32)
    a = np.empty((k // 512, 16))
    for p in range(k // 512):
        a[p, :8] = np.random.permutation(np.resize(levels, 8))
        for g in range(8):
            far = levels[np.abs(levels - a[p, g]) >= 10]
            a[p, g + 8] = far[np.random.randint(len(far))]
    return np.exp2(a.ravel()).repeat(32)


def f64(x):
    return np.asarray(x).astype(np.float64)


def striped(idx):
    return np.tile(np.asarray(idx).reshape(-1, 16).T, (8, 1)).astype(np.uint16)


def unstriped(offs):
    return offs[:16].T.reshape(-1).astype(np.int64)


E2M1 = np.array([0.0, 0.5, 1.0, 1.5, 2.0, 3.0, 4.0, 6.0, -0.0, -0.5, -1.0, -1.5, -2.0, -3.0, -4.0, -6.0])


def pack_weight(w, fmt):
    k, n = w.shape
    w = f64(np.asarray(w, np.float32).astype(ml_dtypes.bfloat16)).reshape(k // 32, 32, n)
    amax = np.abs(w).max(1)
    if fmt == "e4m3":
        byte = np.frexp(amax)[1] - 1 + 127 - 7
    else:
        mant, ex = np.frexp(amax / 6.0)
        byte = np.where(mant > 0.5, ex, ex - 1) + 127
    byte = np.clip(np.where(amax > 0, byte, 1), 1, 254)
    scaled = (w * np.exp2(127.0 - byte)[:, None, :]).reshape(k, n).astype(np.float32)
    by_word = np.ascontiguousarray(scaled.reshape(k // 512, 128, 4, n).transpose(0, 1, 3, 2))
    if fmt == "e4m3":
        words = by_word.astype(ml_dtypes.float8_e4m3fn).view(np.uint8)
    else:
        c = by_word.astype(ml_dtypes.float4_e2m1fn).view(np.uint8) & 0xF
        words = (c[..., 0::2] | (c[..., 1::2] << 4)).reshape(k // 512, 128, 2 * n)
    return np.ascontiguousarray(words), np.ascontiguousarray(byte.astype(np.uint8).reshape(k // 512, 16, n))


def unpack_weight(words, scales, fmt):
    g, _, n = scales.shape
    words = np.ascontiguousarray(words).reshape(g, 128, n, -1)
    if fmt == "e4m3":
        vals = words.view(ml_dtypes.float8_e4m3fn).astype(np.float64)
    else:
        nib = np.empty((g, 128, n, 4), np.uint8)
        nib[..., 0::2] = words & 0xF
        nib[..., 1::2] = words >> 4
        vals = E2M1[nib]
    vals = vals * np.repeat(np.exp2(scales.astype(np.float64) - 127.0), 8, axis=1)[..., None]
    return vals.transpose(0, 1, 3, 2).reshape(g * 512, n)


K, J, T, N = 2048, 512, 512, 512


def setup_inputs():
    n = np.random.standard_normal
    idx = np.random.permutation(K)[:J]
    fk = mx_kscale(K)
    fj = mx_kscale(J)
    tj = np.ones(K)
    tj[idx] = fj
    xo = n((T, K))
    xo[:, idx] *= 6.0
    xr = xo.copy()
    xr[:, idx] = 0.0
    xbp = pack_weight(xr.T / fk[:, None], "e2m1")
    wbp = pack_weight(n((K, N)) * 1 / np.sqrt(K) * fk[:, None], "e2m1")
    wop = pack_weight(n((J, N)) * 1 / np.sqrt(J) * fj[:, None], "e4m3")
    return {
        "xb_words": xbp[0],
        "xb_scales": xbp[1],
        "wb_words": wbp[0],
        "wb_scales": wbp[1],
        "xt": (xo / tj).astype(np.float32),
        "wo_words": wop[0],
        "wo_scales": wop[1],
        "offs": striped(idx),
    }


def reference(xb_words, xb_scales, wb_words, wb_scales, xt, wo_words, wo_scales, offs):
    idx = unstriped(offs)
    xbu = unpack_weight(xb_words, xb_scales, "e2m1")
    wbu = unpack_weight(wb_words, wb_scales, "e2m1")
    wou = unpack_weight(wo_words, wo_scales, "e4m3")
    xo = f64(xt)[:, idx].T
    xoq = mxq(xo, 0, "e4m3")
    y = wbu.T @ xbu + wou.T @ xoq
    return y

@@ -1,0 +1,142 @@
+from contextlib import ExitStack
+
+import concourse.mybir as mybir
+from concourse.masks import make_identity
+
+K, J, T, N = 2048, 512, 512, 512
+FLOPS = 2 * (K + J) * T * N
+
+F32 = mybir.dt.float32
+BF16 = mybir.dt.bfloat16
+I32 = mybir.dt.int32
+U32 = mybir.dt.uint32
+U16 = mybir.dt.uint16
+U8 = mybir.dt.uint8
+FP8X4 = mybir.dt.float8_e4m3fn_x4
+FP4X4 = mybir.dt.float4_e2m1fn_x4
+
+P = 128
+PACK = 4
+PASSES = K // (P * PACK)
+TILES = T // P
+N_TILES = N // P
+
+
+def load_scale_rows(queue, plane, scales):
+    for r in range(4):
+        queue.dma_start(
+            out=plane[r:P:32, :, :].bitcast(I32),
+            in_=scales[:, r:16:4, :].rearrange("z q c -> q z c").bitcast(I32),
+        )
+
+
+def tile_list_outlier_channels_kernel(
+    tc, xb_words, xb_scales, wb_words, wb_scales, xt, wo_words, wo_scales, offs, out
+):
+    nc = tc.nc
+    with ExitStack() as ctx:
+        keep = ctx.enter_context(tc.tile_pool(name="keep", bufs=1))
+        psum = ctx.enter_context(tc.psum_pool(name="psum", bufs=1))
+        turn = ctx.enter_context(tc.psum_pool(name="turn", bufs=2))
+
+        offsets = keep.tile([P, J // 16], U16, name="offsets")
+        wb_codes = keep.tile([P, PASSES, 2 * N], U8, name="wb_codes", align_bytes=64)
+        xb_codes = keep.tile([P, PASSES, 2 * T], U8, name="xb_codes", align_bytes=64)
+        wo_codes = keep.tile([P, N], U32, name="wo_codes", align_bytes=64)
+        wb_plane = keep.tile([P, PASSES, N], U8, name="wb_plane", align_bytes=64)
+        xb_plane = keep.tile([P, PASSES, T], U8, name="xb_plane", align_bytes=64)
+        wo_plane = keep.tile([P, 1, N], U8, name="wo_plane", align_bytes=64)
+        xo_codes = keep.tile([P, T], U32, name="xo_codes", align_bytes=64)
+        xo_plane = keep.tile([P, T], U8, name="xo_plane", align_bytes=64)
+        rows = [keep.tile([P, K], F32, name="rows%d" % i) for i in range(TILES)]
+        ident = keep.tile([P, P], F32, name="ident")
+
+        make_identity(nc, ident[:])
+        for plane in (wb_plane, xb_plane, wo_plane):
+            nc.vector.memset(plane[:].bitcast(I32), 0)
+
+        nc.sync.dma_start(out=wb_codes[:].bitcast(I32), in_=wb_words.rearrange("z p c -> p z c").bitcast(I32))
+        nc.sync.dma_start(out=xb_codes[:].bitcast(I32), in_=xb_words.rearrange("z p c -> p z c").bitcast(I32))
+        for i in range(TILES):
+            if i == TILES - 1:
+                nc.sync.dma_start(
+                    out=wo_codes[:].bitcast(I32),
+                    in_=wo_words[0].rearrange("p n r -> p (n r)").bitcast(I32),
+                )
+            nc.sync.dma_start(out=rows[i][:], in_=xt[i * P : (i + 1) * P, :])
+            if i == 0:
+                nc.sync.dma_start(offsets[:], offs)
+        load_scale_rows(nc.scalar, wb_plane, wb_scales)
+        load_scale_rows(nc.scalar, xb_plane, xb_scales)
+        load_scale_rows(nc.scalar, wo_plane, wo_scales)
+
+        picked = [keep.tile([P, J], BF16, name="picked%d" % i) for i in range(TILES)]
+
+        def gather(i):
+            nc.vector.tensor_copy(picked[i][:], rows[i][:].indirect(offsets[:]))
+
+        def quantize(i):
+            cols = slice(i * P, (i + 1) * P)
+            pairs = picked[i][:].bitcast(F32)
+            turned = turn.tile([P, 2, P], F32, name="turned")
+            for u in range(2):
+                nc.tensor.transpose(turned[:, u, :], pairs[:, u : J // 2 : 2], ident[:])
+            grouped = keep.tile([P, P * PACK], BF16, name="grouped%d" % i, align_bytes=64)
+            nc.scalar.copy(
+                out=grouped[:].bitcast(F32).rearrange("p (t u) -> p t u", u=2),
+                in_=turned[:].rearrange("p u t -> p t u"),
+            )
+            nc.vector.quantize_mx(out=xo_codes[:, cols].bitcast(FP8X4), scales=xo_plane[:, cols], in_=grouped[:])
+
+        parts = [
+            (0, 256, 0, 2, nc.scalar, nc.sync),
+            (0, 256, 2, 2, nc.vector, nc.sync),
+            (256, 128, 0, 4, nc.scalar, nc.sync),
+            (384, 128, 0, 2, nc.vector, nc.sync),
+            (384, 128, 2, 2, nc.scalar, nc.scalar),
+        ]
+        banks = [psum.tile([P, part[3], part[1]], F32, name="bank%d" % a) for a, part in enumerate(parts)]
+
+        def base_pass(z):
+            for b in range(N_TILES):
+                for bank, (t0, width, b0, count, engine, queue) in zip(banks, parts):
+                    if b0 <= b < b0 + count:
+                        nc.tensor.matmul_mx(
+                            out=bank[:, b - b0, :],
+                            lhsT=wb_codes[:, z, 2 * b * P : 2 * (b + 1) * P].bitcast(FP4X4),
+                            lhsT_scale=wb_plane[:, z, b * P : (b + 1) * P],
+                            rhs=xb_codes[:, z, 2 * t0 : 2 * (t0 + width)].bitcast(FP4X4),
+                            rhs_scale=xb_plane[:, z, t0 : t0 + width],
+                            start=(z == 0 and b == b0),
+                            stop=False,
+                        )
+
+        for i in range(TILES):
+            gather(i)
+        base_pass(0)
+        base_pass(1)
+        quantize(0)
+        base_pass(2)
+        quantize(1)
+        base_pass(3)
+        quantize(2)
+        quantize(3)
+
+        out_tiles = out.rearrange("(b p) t -> p b t", p=P)
+        for a, (bank, (t0, width, b0, count, engine, queue)) in enumerate(zip(banks, parts)):
+            for b in range(b0, b0 + count):
+                nc.tensor.matmul_mx(
+                    out=bank[:, b - b0, :],
+                    lhsT=wo_codes[:, b * P : (b + 1) * P].bitcast(FP8X4),
+                    lhsT_scale=wo_plane[:, 0, b * P : (b + 1) * P],
+                    rhs=xo_codes[:, t0 : t0 + width].bitcast(FP8X4),
+                    rhs_scale=xo_plane[:, t0 : t0 + width],
+                    start=False,
+                    stop=(b == b0 + count - 1),
+                )
+            result = keep.tile([P, count, width], F32, name="result%d" % a)
+            if a in (1, 3):
+                nc.vector.tensor_copy(out=result[:], in_=bank[:])
+            else:
+                nc.scalar.copy(out=result[:], in_=bank[:])
+            queue.dma_start(out=out_tiles[:, b0 : b0 + count, t0 : t0 + width], in_=result[:])

@@ -22,8 +22,8 @@ TILES = T // P
 N_TILES = N // P
 
 
-def load_scale_rows(queue, plane, scales):
-    for r in range(4):
+def load_scale_rows(queue, plane, scales, live_rows):
+    for r in live_rows:
         queue.dma_start(
             out=plane[r:P:32, :, :].bitcast(I32),
             in_=scales[:, r:16:4, :].rearrange("z q c -> q z c").bitcast(I32),
@@ -48,27 +48,28 @@ def tile_list_outlier_channels_kernel(
         wo_plane = keep.tile([P, 1, N], U8, name="wo_plane", align_bytes=64)
         xo_codes = keep.tile([P, T], U32, name="xo_codes", align_bytes=64)
         xo_plane = keep.tile([P, T], U8, name="xo_plane", align_bytes=64)
-        rows = [keep.tile([P, K], F32, name="rows%d" % i) for i in range(TILES)]
+        rows = [keep.tile([P, K], F32, name="rows%d" % i, tag="rows%d" % i, align_bytes=64) for i in range(TILES)]
         ident = keep.tile([P, P], F32, name="ident")
 
-        make_identity(nc, ident[:])
+        ident_narrow = keep.tile([P, P], BF16, name="ident_narrow")
+        make_identity(nc, ident_narrow[:])
+        nc.scalar.copy(out=ident[:], in_=ident_narrow[:])
         for plane in (wb_plane, xb_plane, wo_plane):
             nc.vector.memset(plane[:].bitcast(I32), 0)
 
         nc.sync.dma_start(out=wb_codes[:].bitcast(I32), in_=wb_words.rearrange("z p c -> p z c").bitcast(I32))
+        load_scale_rows(nc.sync, wb_plane, wb_scales, range(4))
+        load_scale_rows(nc.sync, xb_plane, xb_scales, range(1))
         nc.sync.dma_start(out=xb_codes[:].bitcast(I32), in_=xb_words.rearrange("z p c -> p z c").bitcast(I32))
-        for i in range(TILES):
-            if i == TILES - 1:
-                nc.sync.dma_start(
-                    out=wo_codes[:].bitcast(I32),
-                    in_=wo_words[0].rearrange("p n r -> p (n r)").bitcast(I32),
-                )
-            nc.sync.dma_start(out=rows[i][:], in_=xt[i * P : (i + 1) * P, :])
-            if i == 0:
-                nc.sync.dma_start(offsets[:], offs)
-        load_scale_rows(nc.scalar, wb_plane, wb_scales)
-        load_scale_rows(nc.scalar, xb_plane, xb_scales)
-        load_scale_rows(nc.scalar, wo_plane, wo_scales)
+        nc.sync.dma_start(out=rows[0][:, : K // 2], in_=xt[0:P, : K // 2])
+        load_scale_rows(nc.sync, xb_plane, xb_scales, range(1, 4))
+        nc.sync.dma_start(out=rows[0][:, K // 2 :], in_=xt[0:P, K // 2 :])
+        nc.sync.dma_start(offsets[:], offs)
+        nc.sync.dma_start(out=rows[1][:], in_=xt[P : 2 * P, :])
+        load_scale_rows(nc.sync, wo_plane, wo_scales, range(4))
+        nc.sync.dma_start(out=rows[2][:], in_=xt[2 * P : 3 * P, :])
+        nc.sync.dma_start(out=wo_codes[:].bitcast(I32), in_=wo_words[0].rearrange("p n r -> p (n r)").bitcast(I32))
+        nc.sync.dma_start(out=rows[3][:], in_=xt[3 * P : 4 * P, :])
 
         picked = [keep.tile([P, J], BF16, name="picked%d" % i) for i in range(TILES)]
 
@@ -81,52 +82,37 @@ def tile_list_outlier_channels_kernel(
             turned = turn.tile([P, 2, P], F32, name="turned")
             for u in range(2):
                 nc.tensor.transpose(turned[:, u, :], pairs[:, u : J // 2 : 2], ident[:])
-            grouped = keep.tile([P, P * PACK], BF16, name="grouped%d" % i, align_bytes=64)
+            tag = "rows%d" % (i + 1) if i < 2 else "grouped%d" % i
+            grouped = keep.tile([P, P * PACK], BF16, name="grouped%d" % i, tag=tag, align_bytes=64)
             nc.scalar.copy(
                 out=grouped[:].bitcast(F32).rearrange("p (t u) -> p t u", u=2),
                 in_=turned[:].rearrange("p u t -> p t u"),
             )
             nc.vector.quantize_mx(out=xo_codes[:, cols].bitcast(FP8X4), scales=xo_plane[:, cols], in_=grouped[:])
 
-        parts = [
-            (0, 256, 0, 2, nc.scalar, nc.sync),
-            (0, 256, 2, 2, nc.vector, nc.sync),
-            (256, 128, 0, 4, nc.scalar, nc.sync),
-            (384, 128, 0, 2, nc.vector, nc.sync),
-            (384, 128, 2, 2, nc.scalar, nc.scalar),
-        ]
+        parts = [(0, 256, 0, 2), (0, 256, 2, 2), (256, 128, 0, 4), (384, 128, 0, 2), (384, 128, 2, 2)]
         banks = [psum.tile([P, part[3], part[1]], F32, name="bank%d" % a) for a, part in enumerate(parts)]
-
-        def base_pass(z):
-            for b in range(N_TILES):
-                for bank, (t0, width, b0, count, engine, queue) in zip(banks, parts):
-                    if b0 <= b < b0 + count:
-                        nc.tensor.matmul_mx(
-                            out=bank[:, b - b0, :],
-                            lhsT=wb_codes[:, z, 2 * b * P : 2 * (b + 1) * P].bitcast(FP4X4),
-                            lhsT_scale=wb_plane[:, z, b * P : (b + 1) * P],
-                            rhs=xb_codes[:, z, 2 * t0 : 2 * (t0 + width)].bitcast(FP4X4),
-                            rhs_scale=xb_plane[:, z, t0 : t0 + width],
-                            start=(z == 0 and b == b0),
-                            stop=False,
-                        )
-
-        for i in range(TILES):
-            gather(i)
-        base_pass(0)
-        base_pass(1)
-        quantize(0)
-        base_pass(2)
-        quantize(1)
-        base_pass(3)
-        quantize(2)
-        quantize(3)
-
         out_tiles = out.rearrange("(b p) t -> p b t", p=P)
-        for a, (bank, (t0, width, b0, count, engine, queue)) in enumerate(zip(banks, parts)):
+
+        def base_passes(a, passes):
+            t0, width, b0, count = parts[a]
+            for z in passes:
+                for b in range(b0, b0 + count):
+                    nc.tensor.matmul_mx(
+                        out=banks[a][:, b - b0, :],
+                        lhsT=wb_codes[:, z, 2 * b * P : 2 * (b + 1) * P].bitcast(FP4X4),
+                        lhsT_scale=wb_plane[:, z, b * P : (b + 1) * P],
+                        rhs=xb_codes[:, z, 2 * t0 : 2 * (t0 + width)].bitcast(FP4X4),
+                        rhs_scale=xb_plane[:, z, t0 : t0 + width],
+                        start=(z == 0 and b == b0),
+                        stop=False,
+                    )
+
+        def finish(a, copy, queue):
+            t0, width, b0, count = parts[a]
             for b in range(b0, b0 + count):
                 nc.tensor.matmul_mx(
-                    out=bank[:, b - b0, :],
+                    out=banks[a][:, b - b0, :],
                     lhsT=wo_codes[:, b * P : (b + 1) * P].bitcast(FP8X4),
                     lhsT_scale=wo_plane[:, 0, b * P : (b + 1) * P],
                     rhs=xo_codes[:, t0 : t0 + width].bitcast(FP8X4),
@@ -135,8 +121,20 @@ def tile_list_outlier_channels_kernel(
                     stop=(b == b0 + count - 1),
                 )
             result = keep.tile([P, count, width], F32, name="result%d" % a)
-            if a in (1, 3):
-                nc.vector.tensor_copy(out=result[:], in_=bank[:])
-            else:
-                nc.scalar.copy(out=result[:], in_=bank[:])
+            copy(out=result[:], in_=banks[a][:])
             queue.dma_start(out=out_tiles[:, b0 : b0 + count, t0 : t0 + width], in_=result[:])
+
+        for i in range(TILES):
+            gather(i)
+        base_passes(0, range(PASSES))
+        for i in range(TILES):
+            quantize(i)
+        base_passes(1, range(PASSES))
+        base_passes(2, range(PASSES))
+        finish(0, nc.scalar.copy, nc.sync)
+        finish(1, nc.scalar.copy, nc.sync)
+        finish(2, nc.scalar.copy, nc.sync)
+        base_passes(3, range(PASSES))
+        base_passes(4, range(PASSES))
+        finish(3, nc.vector.tensor_copy, nc.sync)
+        finish(4, nc.scalar.copy, nc.scalar)

@@ -20,12 +20,13 @@ PACK = 4
 PASSES = K // (P * PACK)
 TILES = T // P
 N_TILES = N // P
+WO_ROW = 4
 
 
-def load_scale_rows(queue, plane, scales, live_rows):
+def load_scale_rows(queue, plane, first_row, scales, live_rows):
     for r in live_rows:
         queue.dma_start(
-            out=plane[r:P:32, :, :].bitcast(I32),
+            out=plane[first_row + r : P : 32, :, :].bitcast(I32),
             in_=scales[:, r:16:4, :].rearrange("z q c -> q z c").bitcast(I32),
         )
 
@@ -37,7 +38,6 @@ def tile_list_outlier_channels_kernel(
     with ExitStack() as ctx:
         keep = ctx.enter_context(tc.tile_pool(name="keep", bufs=1))
         psum = ctx.enter_context(tc.psum_pool(name="psum", bufs=1))
-        turn = ctx.enter_context(tc.psum_pool(name="turn", bufs=2))
 
         offsets = keep.tile([P, J // 16], U16, name="offsets")
         wb_codes = keep.tile([P, PASSES, 2 * N], U8, name="wb_codes", align_bytes=64)
@@ -46,32 +46,34 @@ def tile_list_outlier_channels_kernel(
         wb_plane = keep.tile([P, PASSES, N], U8, name="wb_plane", align_bytes=64)
         xb_plane = keep.tile([P, PASSES, T], U8, name="xb_plane", align_bytes=64)
         wo_plane = keep.tile([P, 1, N], U8, name="wo_plane", align_bytes=64)
-        xo_codes = keep.tile([P, T], U32, name="xo_codes", align_bytes=64)
         xo_plane = keep.tile([P, T], U8, name="xo_plane", align_bytes=64)
         rows = [keep.tile([P, K], F32, name="rows%d" % i, tag="rows%d" % i, align_bytes=64) for i in range(TILES)]
         ident = keep.tile([P, P], F32, name="ident")
 
-        ident_narrow = keep.tile([P, P], BF16, name="ident_narrow")
-        make_identity(nc, ident_narrow[:])
-        nc.scalar.copy(out=ident[:], in_=ident_narrow[:])
         for plane in (wb_plane, xb_plane, wo_plane):
             nc.vector.memset(plane[:].bitcast(I32), 0)
 
         nc.sync.dma_start(out=wb_codes[:].bitcast(I32), in_=wb_words.rearrange("z p c -> p z c").bitcast(I32))
-        load_scale_rows(nc.sync, wb_plane, wb_scales, range(4))
-        load_scale_rows(nc.sync, xb_plane, xb_scales, range(1))
+        load_scale_rows(nc.sync, wb_plane, 0, wb_scales, range(4))
+        load_scale_rows(nc.sync, xb_plane, 0, xb_scales, range(1))
         nc.sync.dma_start(out=xb_codes[:].bitcast(I32), in_=xb_words.rearrange("z p c -> p z c").bitcast(I32))
-        nc.sync.dma_start(out=rows[0][:, : K // 2], in_=xt[0:P, : K // 2])
-        load_scale_rows(nc.sync, xb_plane, xb_scales, range(1, 4))
-        nc.sync.dma_start(out=rows[0][:, K // 2 :], in_=xt[0:P, K // 2 :])
+        nc.sync.dma_start(out=wo_codes[:].bitcast(I32), in_=wo_words[0].rearrange("p n r -> p (n r)").bitcast(I32))
+        load_scale_rows(nc.sync, xb_plane, 0, xb_scales, range(1, 4))
+        nc.sync.dma_start(out=rows[0][:], in_=xt[0:P, :])
         nc.sync.dma_start(offsets[:], offs)
         nc.sync.dma_start(out=rows[1][:], in_=xt[P : 2 * P, :])
-        load_scale_rows(nc.sync, wo_plane, wo_scales, range(4))
+        load_scale_rows(nc.sync, wo_plane, WO_ROW, wo_scales, range(4))
         nc.sync.dma_start(out=rows[2][:], in_=xt[2 * P : 3 * P, :])
-        nc.sync.dma_start(out=wo_codes[:].bitcast(I32), in_=wo_words[0].rearrange("p n r -> p (n r)").bitcast(I32))
         nc.sync.dma_start(out=rows[3][:], in_=xt[3 * P : 4 * P, :])
 
+        ident_narrow = keep.tile([P, P], BF16, name="ident_narrow")
+        make_identity(nc, ident_narrow[:])
+        nc.scalar.copy(out=ident[:], in_=ident_narrow[:])
+
         picked = [keep.tile([P, J], BF16, name="picked%d" % i) for i in range(TILES)]
+
+        early_codes = keep.tile([P, 2 * P], U32, name="early_codes", align_bytes=64)
+        xo_codes = {0: early_codes}
 
         def gather(i):
             nc.vector.tensor_copy(picked[i][:], rows[i][:].indirect(offsets[:]))
@@ -79,23 +81,31 @@ def tile_list_outlier_channels_kernel(
         def quantize(i):
             cols = slice(i * P, (i + 1) * P)
             pairs = picked[i][:].bitcast(F32)
-            turned = turn.tile([P, 2, P], F32, name="turned")
+            turned = psum.tile([P, 2, P], F32, name="turned%d" % i, tag="turned%d" % i)
             for u in range(2):
                 nc.tensor.transpose(turned[:, u, :], pairs[:, u : J // 2 : 2], ident[:])
-            tag = "rows%d" % (i + 1) if i < 2 else "grouped%d" % i
+            tag = "rows1" if i == 0 else "grouped%d" % i
             grouped = keep.tile([P, P * PACK], BF16, name="grouped%d" % i, tag=tag, align_bytes=64)
             nc.scalar.copy(
                 out=grouped[:].bitcast(F32).rearrange("p (t u) -> p t u", u=2),
                 in_=turned[:].rearrange("p u t -> p t u"),
             )
-            nc.vector.quantize_mx(out=xo_codes[:, cols].bitcast(FP8X4), scales=xo_plane[:, cols], in_=grouped[:])
+            if i < 2:
+                codes = early_codes[:, cols]
+            else:
+                tag = "rows3" if i == 2 else "last_codes"
+                xo_codes[i * P] = keep.tile([P, P], U32, name="codes%d" % i, tag=tag, align_bytes=64)
+                codes = xo_codes[i * P][:]
+            nc.vector.quantize_mx(out=codes.bitcast(FP8X4), scales=xo_plane[:, cols], in_=grouped[:])
 
         parts = [(0, 256, 0, 2), (0, 256, 2, 2), (256, 128, 0, 4), (384, 128, 0, 2), (384, 128, 2, 2)]
-        banks = [psum.tile([P, part[3], part[1]], F32, name="bank%d" % a) for a, part in enumerate(parts)]
+        banks = {}
         out_tiles = out.rearrange("(b p) t -> p b t", p=P)
 
         def base_passes(a, passes):
             t0, width, b0, count = parts[a]
+            tag = "bank%d" % a if a < 3 else "turned%d" % (a - 3)
+            banks[a] = psum.tile([P, count, width], F32, name="bank%d" % a, tag=tag)
             for z in passes:
                 for b in range(b0, b0 + count):
                     nc.tensor.matmul_mx(
@@ -114,8 +124,8 @@ def tile_list_outlier_channels_kernel(
                 nc.tensor.matmul_mx(
                     out=banks[a][:, b - b0, :],
                     lhsT=wo_codes[:, b * P : (b + 1) * P].bitcast(FP8X4),
-                    lhsT_scale=wo_plane[:, 0, b * P : (b + 1) * P],
-                    rhs=xo_codes[:, t0 : t0 + width].bitcast(FP8X4),
+                    lhsT_scale=wo_plane[WO_ROW:P, 0, b * P : (b + 1) * P],
+                    rhs=xo_codes[t0][:].bitcast(FP8X4),
                     rhs_scale=xo_plane[:, t0 : t0 + width],
                     start=False,
                     stop=(b == b0 + count - 1),

from contextlib import ExitStack

import concourse.mybir as mybir
from concourse.masks import make_identity

K, J, T, N = 2048, 512, 512, 512
FLOPS = 2 * (K + J) * T * N

F32 = mybir.dt.float32
BF16 = mybir.dt.bfloat16
I32 = mybir.dt.int32
U32 = mybir.dt.uint32
U16 = mybir.dt.uint16
U8 = mybir.dt.uint8
FP8X4 = mybir.dt.float8_e4m3fn_x4
FP4X4 = mybir.dt.float4_e2m1fn_x4

P = 128
PACK = 4
PASSES = K // (P * PACK)
TILES = T // P
N_TILES = N // P
WO_ROW = 4


def load_scale_rows(queue, plane, first_row, scales, live_rows):
    for r in live_rows:
        queue.dma_start(
            out=plane[first_row + r : P : 32, :, :].bitcast(I32),
            in_=scales[:, r:16:4, :].rearrange("z q c -> q z c").bitcast(I32),
        )


def tile_list_outlier_channels_kernel(
    tc, xb_words, xb_scales, wb_words, wb_scales, xt, wo_words, wo_scales, offs, out
):
    nc = tc.nc
    with ExitStack() as ctx:
        keep = ctx.enter_context(tc.tile_pool(name="keep", bufs=1))
        psum = ctx.enter_context(tc.psum_pool(name="psum", bufs=1))

        offsets = keep.tile([P, J // 16], U16, name="offsets")
        wb_codes = keep.tile([P, PASSES, 2 * N], U8, name="wb_codes", align_bytes=64)
        xb_codes = keep.tile([P, PASSES, 2 * T], U8, name="xb_codes", align_bytes=64)
        wo_codes = keep.tile([P, N], U32, name="wo_codes", align_bytes=64)
        wb_plane = keep.tile([P, PASSES, N], U8, name="wb_plane", align_bytes=64)
        xb_plane = keep.tile([P, PASSES, T], U8, name="xb_plane", align_bytes=64)
        wo_plane = keep.tile([P, 1, N], U8, name="wo_plane", align_bytes=64)
        xo_plane = keep.tile([P, T], U8, name="xo_plane", align_bytes=64)
        rows = [keep.tile([P, K], F32, name="rows%d" % i, tag="rows%d" % i, align_bytes=64) for i in range(TILES)]
        ident = keep.tile([P, P], F32, name="ident")

        for plane in (wb_plane, xb_plane, wo_plane):
            nc.vector.memset(plane[:].bitcast(I32), 0)

        nc.sync.dma_start(out=wb_codes[:].bitcast(I32), in_=wb_words.rearrange("z p c -> p z c").bitcast(I32))
        load_scale_rows(nc.sync, wb_plane, 0, wb_scales, range(4))
        load_scale_rows(nc.sync, xb_plane, 0, xb_scales, range(1))
        nc.sync.dma_start(out=xb_codes[:].bitcast(I32), in_=xb_words.rearrange("z p c -> p z c").bitcast(I32))
        nc.sync.dma_start(out=wo_codes[:].bitcast(I32), in_=wo_words[0].rearrange("p n r -> p (n r)").bitcast(I32))
        load_scale_rows(nc.sync, xb_plane, 0, xb_scales, range(1, 4))
        nc.sync.dma_start(out=rows[0][:], in_=xt[0:P, :])
        nc.sync.dma_start(offsets[:], offs)
        nc.sync.dma_start(out=rows[1][:], in_=xt[P : 2 * P, :])
        load_scale_rows(nc.sync, wo_plane, WO_ROW, wo_scales, range(4))
        nc.sync.dma_start(out=rows[2][:], in_=xt[2 * P : 3 * P, :])
        nc.sync.dma_start(out=rows[3][:], in_=xt[3 * P : 4 * P, :])

        ident_narrow = keep.tile([P, P], BF16, name="ident_narrow")
        make_identity(nc, ident_narrow[:])
        nc.scalar.copy(out=ident[:], in_=ident_narrow[:])

        picked = [keep.tile([P, J], BF16, name="picked%d" % i) for i in range(TILES)]

        early_codes = keep.tile([P, 2 * P], U32, name="early_codes", align_bytes=64)
        xo_codes = {0: early_codes}

        def gather(i):
            nc.vector.tensor_copy(picked[i][:], rows[i][:].indirect(offsets[:]))

        def quantize(i):
            cols = slice(i * P, (i + 1) * P)
            pairs = picked[i][:].bitcast(F32)
            turned = psum.tile([P, 2, P], F32, name="turned%d" % i, tag="turned%d" % i)
            for u in range(2):
                nc.tensor.transpose(turned[:, u, :], pairs[:, u : J // 2 : 2], ident[:])
            tag = "rows1" if i == 0 else "grouped%d" % i
            grouped = keep.tile([P, P * PACK], BF16, name="grouped%d" % i, tag=tag, align_bytes=64)
            nc.scalar.copy(
                out=grouped[:].bitcast(F32).rearrange("p (t u) -> p t u", u=2),
                in_=turned[:].rearrange("p u t -> p t u"),
            )
            if i < 2:
                codes = early_codes[:, cols]
            else:
                tag = "rows3" if i == 2 else "last_codes"
                xo_codes[i * P] = keep.tile([P, P], U32, name="codes%d" % i, tag=tag, align_bytes=64)
                codes = xo_codes[i * P][:]
            nc.vector.quantize_mx(out=codes.bitcast(FP8X4), scales=xo_plane[:, cols], in_=grouped[:])

        parts = [(0, 256, 0, 2), (0, 256, 2, 2), (256, 128, 0, 4), (384, 128, 0, 2), (384, 128, 2, 2)]
        banks = {}
        out_tiles = out.rearrange("(b p) t -> p b t", p=P)

        def base_passes(a, passes):
            t0, width, b0, count = parts[a]
            tag = "bank%d" % a if a < 3 else "turned%d" % (a - 3)
            banks[a] = psum.tile([P, count, width], F32, name="bank%d" % a, tag=tag)
            for z in passes:
                for b in range(b0, b0 + count):
                    nc.tensor.matmul_mx(
                        out=banks[a][:, b - b0, :],
                        lhsT=wb_codes[:, z, 2 * b * P : 2 * (b + 1) * P].bitcast(FP4X4),
                        lhsT_scale=wb_plane[:, z, b * P : (b + 1) * P],
                        rhs=xb_codes[:, z, 2 * t0 : 2 * (t0 + width)].bitcast(FP4X4),
                        rhs_scale=xb_plane[:, z, t0 : t0 + width],
                        start=(z == 0 and b == b0),
                        stop=False,
                    )

        def finish(a, copy, queue):
            t0, width, b0, count = parts[a]
            for b in range(b0, b0 + count):
                nc.tensor.matmul_mx(
                    out=banks[a][:, b - b0, :],
                    lhsT=wo_codes[:, b * P : (b + 1) * P].bitcast(FP8X4),
                    lhsT_scale=wo_plane[WO_ROW:P, 0, b * P : (b + 1) * P],
                    rhs=xo_codes[t0][:].bitcast(FP8X4),
                    rhs_scale=xo_plane[:, t0 : t0 + width],
                    start=False,
                    stop=(b == b0 + count - 1),
                )
            result = keep.tile([P, count, width], F32, name="result%d" % a)
            copy(out=result[:], in_=banks[a][:])
            queue.dma_start(out=out_tiles[:, b0 : b0 + count, t0 : t0 + width], in_=result[:])

        for i in range(TILES):
            gather(i)
        base_passes(0, range(PASSES))
        for i in range(TILES):
            quantize(i)
        base_passes(1, range(PASSES))
        base_passes(2, range(PASSES))
        finish(0, nc.scalar.copy, nc.sync)
        finish(1, nc.scalar.copy, nc.sync)
        finish(2, nc.scalar.copy, nc.sync)
        base_passes(3, range(PASSES))
        base_passes(4, range(PASSES))
        finish(3, nc.vector.tensor_copy, nc.sync)
        finish(4, nc.scalar.copy, nc.scalar)
